import numpy as np
import ml_dtypes


def mxq(x, axis, fmt="e4m3"):
    dtype, down = {"e4m3": (ml_dtypes.float8_e4m3fn, 7), "e5m2": (ml_dtypes.float8_e5m2, 14)}[fmt]
    v = np.moveaxis(np.asarray(x, np.float32).astype(ml_dtypes.bfloat16).astype(np.float64), axis, -1)
    blocks = v.reshape(v.shape[:-1] + (-1, 32))
    amax = np.abs(blocks).max(-1, keepdims=True)
    byte = np.maximum(np.where(amax > 0, np.frexp(amax)[1] - 1 + 127, 0) - down, 1)
    scale = np.exp2(byte - 127.0)
    codes = (blocks / scale).astype(np.float32).astype(dtype).astype(np.float64)
    return np.moveaxis((codes * scale).reshape(v.shape), -1, axis)


WIDE = False


def mx_kscale(k):
    if not WIDE:
        return np.ones(k)
    levels = np.array([10, -10, 5, -5, 0])
    if k % 512:
        return np.exp2(np.random.permutation(np.resize(levels, k // 32))).repeat(32)
    a = np.empty((k // 512, 16))
    for p in range(k // 512):
        a[p, :8] = np.random.permutation(np.resize(levels, 8))
        for g in range(8):
            far = levels[np.abs(levels - a[p, g]) >= 10]
            a[p, g + 8] = far[np.random.randint(len(far))]
    return np.exp2(a.ravel()).repeat(32)


def f64(x):
    return np.asarray(x).astype(np.float64)


def striped(idx):
    return np.tile(idx.reshape(-1, 16).T, (8, 1)).astype(np.uint16)


def unstriped(offs):
    return offs[:16].T.reshape(-1).astype(np.int64)


E2M1 = np.array([0.0, 0.5, 1.0, 1.5, 2.0, 3.0, 4.0, 6.0, -0.0, -0.5, -1.0, -1.5, -2.0, -3.0, -4.0, -6.0])


def pack_weight(w, fmt):
    k, n = w.shape
    w = f64(np.asarray(w, np.float32).astype(ml_dtypes.bfloat16)).reshape(k // 32, 32, n)
    amax = np.abs(w).max(1)
    if fmt == "e4m3":
        byte = np.frexp(amax)[1] - 1 + 127 - 7
    else:
        mant, ex = np.frexp(amax / 6.0)
        byte = np.where(mant > 0.5, ex, ex - 1) + 127
    byte = np.clip(np.where(amax > 0, byte, 1), 1, 254)
    scaled = (w * np.exp2(127.0 - byte)[:, None, :]).reshape(k, n).astype(np.float32)
    by_word = np.ascontiguousarray(scaled.reshape(k // 512, 128, 4, n).transpose(0, 1, 3, 2))
    if fmt == "e4m3":
        words = by_word.astype(ml_dtypes.float8_e4m3fn).view(np.uint8)
    else:
        c = by_word.astype(ml_dtypes.float4_e2m1fn).view(np.uint8) & 0xF
        words = (c[..., 0::2] | (c[..., 1::2] << 4)).reshape(k // 512, 128, 2 * n)
    return np.ascontiguousarray(words), np.ascontiguousarray(byte.astype(np.uint8).reshape(k // 512, 16, n))


def unpack_weight(words, scales, fmt):
    g, _, n = scales.shape
    words = np.ascontiguousarray(words).reshape(g, 128, n, -1)
    if fmt == "e4m3":
        vals = words.view(ml_dtypes.float8_e4m3fn).astype(np.float64)
    else:
        nib = np.empty((g, 128, n, 4), np.uint8)
        nib[..., 0::2] = words & 0xF
        nib[..., 1::2] = words >> 4
        vals = E2M1[nib]
    vals = vals * np.repeat(np.exp2(scales.astype(np.float64) - 127.0), 8, axis=1)[..., None]
    return vals.transpose(0, 1, 3, 2).reshape(g * 512, n)


def gelu(v):
    return 0.5 * v * (1.0 + np.tanh(np.sqrt(2.0 / np.pi) * (v + 0.044715 * v**3)))


def bf(x):
    return np.asarray(x, np.float32).astype(ml_dtypes.bfloat16)


def planes(Y):
    n, m = Y.shape
    b = f64(bf(Y)).reshape(n // 32, 32, m)
    amax = np.abs(b).max(1)
    byte = np.clip(np.where(amax > 0, np.frexp(amax)[1] - 1 + 127 - 7, 1), 1, 254)
    codes = (b * np.exp2(127.0 - byte)[:, None, :]).reshape(n, m).astype(np.float32).astype(ml_dtypes.float8_e4m3fn).view(np.uint8)
    words = codes.reshape(n // 512, 128, 4, m).transpose(0, 1, 3, 2)
    return np.ascontiguousarray(words), np.ascontiguousarray(byte.astype(np.uint8).reshape(n // 512, 16, m))


K, H, N, T, S, P = 1536, 1024, 512, 4096, 1024, 512

def setup_inputs():
    n = np.random.standard_normal
    s = mx_kscale(K)[:, None]
    u = mx_kscale(H)[:, None]
    d = {}
    d["tab_words"], d["tab_scales"] = pack_weight(n((K, T)) * s, "e4m3")
    d["offs"] = striped(np.random.permutation(T)[:S])
    d["pos1"] = striped(np.random.permutation(S)[:P])
    d["pos2"] = striped(np.random.permutation(S)[:P])
    d["w1"] = (0.5 * n((K, H)) / s / K**0.5).astype(np.float32)
    d["shift"] = np.random.uniform(-0.3, 0.3, H).astype(np.float32)
    d["gain"] = (np.exp(0.3 * n(H)) * u[:, 0]).astype(np.float32)
    d["w2"] = (2.5 * n((H, N)) / u / H**0.5).astype(np.float32)
    d["w3_words"], d["w3_scales"] = pack_weight(n((K, N)) / s / K**0.5, "e2m1")
    d["emph"] = (np.exp(0.8 * n(N))[:, None] * np.exp(0.4 * n((N, P)))).astype(np.float32)
    return d

def reference(tab_words, tab_scales, offs, pos1, pos2, w1, shift, gain, w2, w3_words, w3_scales, emph):
    v = unpack_weight(tab_words, tab_scales, "e4m3")[:, unstriped(offs)]
    arg = (mxq(f64(w1), 0, "e4m3").T @ v) + f64(shift)[:, None]
    h = np.sin(arg) * f64(gain)[:, None]
    mixed = mxq(f64(w2), 0, "e4m3").T @ mxq(h, 0, "e4m3")
    skip = unpack_weight(w3_words, w3_scales, "e2m1").T @ v
    g2 = np.maximum(mixed, skip)
    y = (g2[:, unstriped(pos1)] + g2[:, unstriped(pos2)]) * f64(emph)
    words, scales = planes(y)
    return y, words, scales

@@ -1,0 +1,329 @@
+import math
+from contextlib import ExitStack
+
+import concourse.mybir as mybir
+
+K, H, N, T, S, PAIRS = 1536, 1024, 512, 4096, 1024, 512
+FLOPS = 2 * K * H * S + 2 * H * N * S + 2 * K * N * S
+
+F32 = mybir.dt.float32
+BF16 = mybir.dt.bfloat16
+I32 = mybir.dt.int32
+U32 = mybir.dt.uint32
+U16 = mybir.dt.uint16
+U8 = mybir.dt.uint8
+FP8X4 = mybir.dt.float8_e4m3fn_x4
+FP4X4 = mybir.dt.float4_e2m1fn_x4
+ALU = mybir.AluOpType
+ACT = mybir.ActivationFunctionType
+
+P = 128
+PACK = 4
+K_PASS = P * PACK
+BANK = 512
+KA = K // K_PASS
+HB = H // K_PASS
+JH = S // BANK
+MH = 2
+MW = PAIRS // MH
+TWO_PI = 2.0 * math.pi
+
+
+def tile_list_trampoline_phase_features_kernel(
+    tc, tab_words, tab_scales, offs, pos1, pos2, w1, shift, gain, w2, w3_words, w3_scales, emph, out_0, out_1, out_2
+):
+    nc = tc.nc
+    with ExitStack() as ctx:
+        lists = ctx.enter_context(tc.tile_pool(name="lists", bufs=1))
+        keep = ctx.enter_context(tc.tile_pool(name="keep", bufs=1))
+        ring = ctx.enter_context(tc.tile_pool(name="ring", bufs=2))
+        psum = ctx.enter_context(tc.psum_pool(name="psum", bufs=8))
+
+        offs_t = lists.tile([P, S // 16], U16, name="offs_t")
+        pos1_t = lists.tile([P, PAIRS // 16], U16, name="pos1_t")
+        pos2_t = lists.tile([P, PAIRS // 16], U16, name="pos2_t")
+
+        tab = [keep.tile([P, T], U32, name="tab%d" % a, align_bytes=64) for a in range(KA)]
+        tab_sc = keep.tile([P, T], U8, name="tab_sc", align_bytes=64)
+        v_codes = [keep.tile([P, S], U32, name="v_codes%d" % a, align_bytes=64) for a in range(KA)]
+        v_sc = [keep.tile([P, S], U8, name="v_sc%d" % a, align_bytes=64) for a in range(KA)]
+        w3_raw = keep.tile([P, KA, 2 * N], U8, name="w3_raw", align_bytes=64)
+        w3_sc_raw = keep.tile([P, KA, N], U8, name="w3_sc_raw", align_bytes=64)
+        w3_codes = keep.tile([P, KA, 2 * N], U8, name="w3_codes", align_bytes=64)
+        w3_sc = keep.tile([P, KA, N], U8, name="w3_sc", align_bytes=64)
+        shift_t = keep.tile([P, HB, PACK], F32, name="shift_t")
+        gain_t = keep.tile([P, HB, PACK], F32, name="gain_t")
+        g2 = [keep.tile([P, S], F32, name="g2_%d" % t, align_bytes=64) for t in range(PACK)]
+        warm = keep.tile([P, 2], F32, name="warm")
+
+        nc.gpsimd.memset(tab_sc[:].bitcast(I32), 0)
+        nc.vector.memset(w3_sc_raw[:].rearrange("p a n -> p (a n)").bitcast(I32), 0)
+        for a in range(1, KA):
+            nc.vector.memset(v_sc[a][:].bitcast(I32), 0)
+        nc.vector.memset(warm[:], 0.0)
+        clock = keep.tile([P, 16], F32, name="clock")
+        clock2 = keep.tile([P, 16], U32, name="clock2")
+        nc.scalar.activation(out=warm[:, 1:2], in_=warm[:, 0:1], func=ACT.Sin)
+
+        def load_table(a, c0, c1):
+            words = tab_words[a].rearrange("p t i -> p (t i)").bitcast(I32)
+            nc.sync.dma_start(out=tab[a][:, c0:c1].bitcast(I32), in_=words[:, c0:c1])
+
+        def load_weight(w, k0, c0):
+            raw = ring.tile([P, PACK, BANK], F32, name="raw", tag="raw", bufs=4, align_bytes=64)
+            nc.sync.dma_start(
+                out=raw[:], in_=w[k0 : k0 + K_PASS, c0 : c0 + BANK].rearrange("(p j) c -> p j c", j=PACK)
+            )
+            return raw
+
+        def round_weight(engine, raw, halves):
+            grouped = ring.tile([P, PACK, P, PACK], BF16, name="grouped", tag="grouped", bufs=3, align_bytes=64)
+            step = P // halves
+            for h in range(halves):
+                ms = slice(h * step, (h + 1) * step)
+                src = raw[:].rearrange("p j (m t) -> p m j t", t=PACK)[:, ms]
+                dst = grouped[:].rearrange("p t m j -> p m j t")[:, ms]
+                if engine == "vector":
+                    nc.vector.tensor_copy(out=dst, in_=src)
+                else:
+                    nc.scalar.copy(out=dst, in_=src)
+            return grouped
+
+        def quantise_weight(grouped, name):
+            codes = keep.tile([P, BANK], U32, name=name + "_codes", align_bytes=64)
+            scales = keep.tile([P, BANK], U8, name=name + "_sc", align_bytes=64)
+            nc.vector.quantize_mx(
+                out=codes[:].bitcast(FP8X4), scales=scales[:], in_=grouped[:].rearrange("p t m j -> p (t m j)")
+            )
+            return codes, scales
+
+        load_table(0, 0, T // 2)
+        nc.sync.dma_start(offs_t[:], offs)
+        nc.sync.dma_start(out=shift_t[:], in_=shift.rearrange("(b p t) -> p b t", p=P, t=PACK))
+        nc.sync.dma_start(out=gain_t[:], in_=gain.rearrange("(b p t) -> p b t", p=P, t=PACK))
+        nc.sync.dma_start(pos1_t[:], pos1)
+        nc.sync.dma_start(pos2_t[:], pos2)
+        nc.sync.dma_start(out=w3_raw[:].bitcast(I32), in_=w3_words.rearrange("a p c -> p a c").bitcast(I32))
+        load_table(0, T // 2, T)
+        for q in range(4):
+            nc.sync.dma_start(
+                out=tab_sc[32 * q : 32 * q + 4 * KA, :].bitcast(I32),
+                in_=tab_scales[:, 4 * q : 4 * q + 4, :].bitcast(I32),
+            )
+        load_table(1, 0, T // 2)
+        for q in range(4):
+            nc.sync.dma_start(
+                out=w3_sc_raw[32 * q : 32 * q + 4].bitcast(I32),
+                in_=w3_scales[:, 4 * q : 4 * q + 4, :].rearrange("a r n -> r a n").bitcast(I32),
+            )
+        load_table(1, T // 2, T)
+        load_table(2, 0, T)
+        w1_raw = {}
+        for a in range(KA):
+            w1_raw[(0, a)] = load_weight(w1, a * K_PASS, 0)
+
+        for a in range(KA):
+            nc.vector.tensor_copy(
+                out=w3_codes[:, a, :].rearrange("p (t m b) -> p m t b", t=PACK, b=2),
+                in_=w3_raw[:, a, :].rearrange("p (m t b) -> p m t b", t=PACK, b=2),
+            )
+        nc.vector.tensor_copy(out=v_codes[0][:], in_=tab[0][:].indirect(offs_t[:]))
+        nc.vector.tensor_copy(out=v_sc[0][:], in_=tab_sc[:].indirect(offs_t[:]))
+        for a in range(1, KA):
+            nc.scalar.dma_start(
+                out=v_sc[a][0:112, :].bitcast(I32),
+                in_=v_sc[0][4 * a : 4 * a + 112, :].bitcast(I32),
+            )
+        nc.vector.tensor_copy(
+            out=w3_sc[:].rearrange("p a (t m) -> p a m t", t=PACK),
+            in_=w3_sc_raw[:].rearrange("p a (m t) -> p a m t", t=PACK),
+        )
+        for a in range(1, KA):
+            nc.vector.tensor_copy(out=v_codes[a][:], in_=tab[a][:].indirect(offs_t[:]))
+
+        skip_banks = {}
+        for jh in range(JH):
+            for t in range(PACK):
+                skip_banks[(jh, t)] = psum.tile([P, BANK], F32, name="bank", tag="bank")
+        for a in range(KA):
+            for jh in range(JH):
+                js = slice(jh * BANK, (jh + 1) * BANK)
+                for t in range(PACK):
+                    nc.tensor.matmul_mx(
+                        out=skip_banks[(jh, t)][:],
+                        lhsT=w3_codes[:, a, 2 * P * t : 2 * P * (t + 1)].bitcast(FP4X4),
+                        lhsT_scale=w3_sc[:, a, P * t : P * (t + 1)],
+                        rhs=v_codes[a][:, js].bitcast(FP8X4),
+                        rhs_scale=v_sc[a][:, js],
+                        start=(a == 0),
+                        stop=(a == KA - 1),
+                    )
+        for jh in range(JH):
+            for t in range(PACK):
+                nc.scalar.copy(out=g2[t][:, jh * BANK : (jh + 1) * BANK], in_=skip_banks[(jh, t)][:])
+
+        w1_q = {}
+        for a in range(KA):
+            w1_q[(0, a)] = quantise_weight(round_weight("vector", w1_raw[(0, a)], 1), "w1_0%d" % a)
+        for a in range(KA):
+            w1_raw[(1, a)] = load_weight(w1, a * K_PASS, BANK)
+        w2_raw = [load_weight(w2, b * K_PASS, 0) for b in range(HB)]
+        emph_t = ring.tile([P, PACK, PAIRS], F32, name="emph_t", tag="raw", bufs=4, align_bytes=64)
+        nc.sync.dma_start(out=emph_t[:], in_=emph.rearrange("(p t) m -> p t m", t=PACK))
+
+        h_q = {}
+        w2_q = []
+
+        xs = {}
+        sines_of = {}
+
+        def arguments(b, jh):
+            js = slice(jh * BANK, (jh + 1) * BANK)
+            x = ring.tile([P, PACK, BANK], F32, name="x", tag="x", bufs=2, align_bytes=64)
+            xs[(b, jh)] = x
+            for t in range(PACK):
+                bank = psum.tile([P, BANK], F32, name="bank", tag="bank")
+                for a in range(KA):
+                    codes, scales = w1_q[(b, a)]
+                    nc.tensor.matmul_mx(
+                        out=bank[:],
+                        lhsT=codes[:, P * t : P * (t + 1)].bitcast(FP8X4),
+                        lhsT_scale=scales[:, P * t : P * (t + 1)],
+                        rhs=v_codes[a][:, js].bitcast(FP8X4),
+                        rhs_scale=v_sc[a][:, js],
+                        start=(a == 0),
+                        stop=(a == KA - 1),
+                    )
+                nc.scalar.activation(out=x[:, t, :], in_=bank[:], func=ACT.Identity, bias=shift_t[:, b, t : t + 1])
+                if b == 0 and jh == 0 and t == 0:
+                    nc.gpsimd.tensor_copy(out=clock[:, 0:1], in_=x[:, 0, 0:1])
+
+        def wrap(b, jh):
+            x = xs[(b, jh)]
+            turns = ring.tile([P, PACK, BANK], I32, name="turns", tag="turns", bufs=1, align_bytes=64)
+            for u in range(2):
+                ts = slice(2 * u, 2 * u + 2)
+                nc.vector.tensor_scalar(
+                    out=turns[:, ts, :], in0=x[:, ts, :], scalar1=1.0 / TWO_PI, scalar2=None, op0=ALU.mult
+                )
+            for u in range(2):
+                ts = slice(2 * u, 2 * u + 2)
+                nc.vector.scalar_tensor_tensor(
+                    out=x[:, ts, :], in0=turns[:, ts, :], scalar=-TWO_PI, in1=x[:, ts, :], op0=ALU.mult, op1=ALU.add
+                )
+
+        def sine(b, jh):
+            x = xs[(b, jh)]
+            sines = ring.tile([P, BANK, PACK], F32, name="sines", tag="sines", bufs=2, align_bytes=64)
+            sines_of[(b, jh)] = sines
+            for u in range(2):
+                cs = slice(u * BANK // 8, (u + 1) * BANK // 8)
+                nc.scalar.activation(
+                    out=sines[:].rearrange("p (c i) t -> p c t i", i=4)[:, cs],
+                    in_=x[:].rearrange("p t (c i) -> p c t i", i=4)[:, cs],
+                    func=ACT.Sin,
+                )
+
+        def quantise_h(b, jh):
+            sines = sines_of[(b, jh)]
+            hb = ring.tile([P, BANK, PACK], BF16, name="hb", tag="hb", bufs=2, align_bytes=64)
+            for u in range(2):
+                hs = slice(u * BANK // 2, (u + 1) * BANK // 2)
+                nc.vector.tensor_tensor(
+                    out=hb[:, hs, :],
+                    in0=sines[:, hs, :],
+                    in1=gain_t[:, b, :].unsqueeze(1).to_broadcast([P, BANK // 2, PACK]),
+                    op=ALU.mult,
+                )
+            codes = keep.tile([P, BANK], U32, name="h_codes%d%d" % (b, jh), align_bytes=64)
+            scales = keep.tile([P, BANK], U8, name="h_sc%d%d" % (b, jh), align_bytes=64)
+            nc.vector.quantize_mx(out=codes[:].bitcast(FP8X4), scales=scales[:], in_=hb[:].rearrange("p j t -> p (j t)"))
+            h_q[(b, jh)] = (codes, scales)
+            if b == 1 and jh == 0:
+                nc.gpsimd.tensor_copy(out=clock2[:, 0:1], in_=codes[:, 0:1])
+
+        def mix(jh):
+            js = slice(jh * BANK, (jh + 1) * BANK)
+            for t in range(PACK):
+                bank = psum.tile([P, BANK], F32, name="bank", tag="bank")
+                for b in range(HB):
+                    nc.tensor.matmul_mx(
+                        out=bank[:],
+                        lhsT=w2_q[b][0][:, P * t : P * (t + 1)].bitcast(FP8X4),
+                        lhsT_scale=w2_q[b][1][:, P * t : P * (t + 1)],
+                        rhs=h_q[(b, jh)][0][:].bitcast(FP8X4),
+                        rhs_scale=h_q[(b, jh)][1][:],
+                        start=(b == 0),
+                        stop=(b == HB - 1),
+                    )
+                nc.vector.tensor_tensor(out=g2[t][:, js], in0=bank[:], in1=g2[t][:, js], op=ALU.max)
+
+        def w1_piece(engine, a):
+            w1_q[(1, a)] = quantise_weight(round_weight(engine, w1_raw[(1, a)], 2), "w1_1%d" % a)
+
+        def w2_piece(b):
+            w2_q.append(quantise_weight(round_weight("scalar", w2_raw[b], 2), "w2_%d" % b))
+
+        arguments(0, 0)
+        wrap(0, 0)
+        arguments(0, 1)
+        sine(0, 0)
+        wrap(0, 1)
+        w1_piece("scalar", 0)
+        quantise_h(0, 0)
+        sine(0, 1)
+        w1_piece("scalar", 1)
+        w1_piece("vector", 2)
+        arguments(1, 0)
+        quantise_h(0, 1)
+        wrap(1, 0)
+        w2_piece(0)
+        arguments(1, 1)
+        sine(1, 0)
+        wrap(1, 1)
+        w2_piece(1)
+        quantise_h(1, 0)
+        sine(1, 1)
+        mix(0)
+        quantise_h(1, 1)
+        mix(1)
+
+        y_codes = keep.tile([P, PAIRS], U32, name="y_codes", align_bytes=64)
+        y_sc = keep.tile([P, PAIRS], U8, name="y_sc", align_bytes=64)
+        out_rows = out_0.rearrange("(p t) m -> p t m", t=PACK)
+        out_words = out_1[0].rearrange("p m t -> p (m t)").bitcast(I32)
+        for mh in range(MH):
+            ms = slice(mh * MW, (mh + 1) * MW)
+            ls = slice(mh * MW // 16, (mh + 1) * MW // 16)
+            y = ring.tile([P, PACK, MW], F32, name="y", tag="y", bufs=2, align_bytes=64)
+            for u in range(2):
+                first = []
+                both = []
+                for t in range(2 * u, 2 * u + 2):
+                    take = ring.tile([P, MW], F32, name="take", tag="take", bufs=2, align_bytes=64)
+                    nc.vector.tensor_copy(out=take[:], in_=g2[t][:].indirect(pos1_t[:, ls]))
+                    first.append(take)
+                for t in range(2 * u, 2 * u + 2):
+                    pair = ring.tile([P, MW], F32, name="pair", tag="pair", bufs=2, align_bytes=64)
+                    nc.vector.tensor_tensor(
+                        out=pair[:], in0=g2[t][:].indirect(pos2_t[:, ls]), in1=first[t - 2 * u][:], op=ALU.add
+                    )
+                    both.append(pair)
+                for t in range(2 * u, 2 * u + 2):
+                    nc.vector.tensor_tensor(out=y[:, t, :], in0=both[t - 2 * u][:], in1=emph_t[:, t, ms], op=ALU.mult)
+                nc.sync.dma_start(out=out_rows[:, 2 * u : 2 * u + 2, ms], in_=y[:, 2 * u : 2 * u + 2, :])
+            yb = ring.tile([P, MW, PACK], BF16, name="yb", tag="hb", bufs=2, align_bytes=64)
+            dst = yb[:].rearrange("p (c i) t -> p c t i", i=4)
+            src = y[:].rearrange("p t (c i) -> p c t i", i=4)
+            if mh == MH - 1:
+                nc.vector.tensor_copy(out=dst, in_=src)
+            else:
+                nc.scalar.copy(out=dst, in_=src)
+            nc.vector.quantize_mx(
+                out=y_codes[:, ms].bitcast(FP8X4), scales=y_sc[:, ms], in_=yb[:].rearrange("p m t -> p (m t)")
+            )
+            nc.sync.dma_start(out=out_words[:, ms], in_=y_codes[:, ms].bitcast(I32))
+        for q in range(4):
+            nc.scalar.dma_start(
+                out=out_2[0, 4 * q : 4 * q + 4, :].bitcast(I32), in_=y_sc[32 * q : 32 * q + 4, :].bitcast(I32)
+            )

@@ -37,7 +37,7 @@ def tile_list_trampoline_phase_features_kernel(
         lists = ctx.enter_context(tc.tile_pool(name="lists", bufs=1))
         keep = ctx.enter_context(tc.tile_pool(name="keep", bufs=1))
         ring = ctx.enter_context(tc.tile_pool(name="ring", bufs=2))
-        psum = ctx.enter_context(tc.psum_pool(name="psum", bufs=8))
+        psum = ctx.enter_context(tc.psum_pool(name="psum", bufs=1))
 
         offs_t = lists.tile([P, S // 16], U16, name="offs_t")
         pos1_t = lists.tile([P, PAIRS // 16], U16, name="pos1_t")
@@ -56,13 +56,12 @@ def tile_list_trampoline_phase_features_kernel(
         g2 = [keep.tile([P, S], F32, name="g2_%d" % t, align_bytes=64) for t in range(PACK)]
         warm = keep.tile([P, 2], F32, name="warm")
 
-        nc.gpsimd.memset(tab_sc[:].bitcast(I32), 0)
+        nc.gpsimd.memset(tab_sc[:, : T // 2].bitcast(I32), 0)
+        nc.vector.memset(tab_sc[:, T // 2 :].bitcast(I32), 0)
         nc.vector.memset(w3_sc_raw[:].rearrange("p a n -> p (a n)").bitcast(I32), 0)
         for a in range(1, KA):
             nc.vector.memset(v_sc[a][:].bitcast(I32), 0)
         nc.vector.memset(warm[:], 0.0)
-        clock = keep.tile([P, 16], F32, name="clock")
-        clock2 = keep.tile([P, 16], U32, name="clock2")
         nc.scalar.activation(out=warm[:, 1:2], in_=warm[:, 0:1], func=ACT.Sin)
 
         def load_table(a, c0, c1):
@@ -76,48 +75,47 @@ def tile_list_trampoline_phase_features_kernel(
             )
             return raw
 
-        def round_weight(engine, raw, halves):
-            grouped = ring.tile([P, PACK, P, PACK], BF16, name="grouped", tag="grouped", bufs=3, align_bytes=64)
-            step = P // halves
-            for h in range(halves):
-                ms = slice(h * step, (h + 1) * step)
-                src = raw[:].rearrange("p j (m t) -> p m j t", t=PACK)[:, ms]
-                dst = grouped[:].rearrange("p t m j -> p m j t")[:, ms]
-                if engine == "vector":
-                    nc.vector.tensor_copy(out=dst, in_=src)
-                else:
-                    nc.scalar.copy(out=dst, in_=src)
+        def round_weight(engine, raw, grouped):
+            src = raw[:].rearrange("p j (m t) -> p m j t", t=PACK)
+            dst = grouped.rearrange("p (t m j) -> p m j t", t=PACK, j=PACK)
+            if engine == "vector":
+                nc.vector.tensor_copy(out=dst, in_=src)
+            else:
+                nc.scalar.copy(out=dst, in_=src)
             return grouped
+
+        def rounded_tile(tag, pieces, bufs):
+            return ring.tile([P, pieces * PACK * BANK], BF16, name="grouped", tag=tag, bufs=bufs, align_bytes=64)
 
         def quantise_weight(grouped, name):
             codes = keep.tile([P, BANK], U32, name=name + "_codes", align_bytes=64)
             scales = keep.tile([P, BANK], U8, name=name + "_sc", align_bytes=64)
-            nc.vector.quantize_mx(
-                out=codes[:].bitcast(FP8X4), scales=scales[:], in_=grouped[:].rearrange("p t m j -> p (t m j)")
-            )
+            nc.vector.quantize_mx(out=codes[:].bitcast(FP8X4), scales=scales[:], in_=grouped)
             return codes, scales
 
-        load_table(0, 0, T // 2)
+        half_t = T // 2
+        load_table(0, 0, half_t)
         nc.sync.dma_start(offs_t[:], offs)
+        nc.sync.dma_start(out=w3_raw[:].bitcast(I32), in_=w3_words.rearrange("a p c -> p a c").bitcast(I32))
         nc.sync.dma_start(out=shift_t[:], in_=shift.rearrange("(b p t) -> p b t", p=P, t=PACK))
         nc.sync.dma_start(out=gain_t[:], in_=gain.rearrange("(b p t) -> p b t", p=P, t=PACK))
+        load_table(0, half_t, T)
         nc.sync.dma_start(pos1_t[:], pos1)
         nc.sync.dma_start(pos2_t[:], pos2)
-        nc.sync.dma_start(out=w3_raw[:].bitcast(I32), in_=w3_words.rearrange("a p c -> p a c").bitcast(I32))
-        load_table(0, T // 2, T)
+        load_table(1, 0, half_t)
         for q in range(4):
             nc.sync.dma_start(
                 out=tab_sc[32 * q : 32 * q + 4 * KA, :].bitcast(I32),
                 in_=tab_scales[:, 4 * q : 4 * q + 4, :].bitcast(I32),
             )
-        load_table(1, 0, T // 2)
+        load_table(1, half_t, T)
+        load_table(2, 0, half_t)
         for q in range(4):
             nc.sync.dma_start(
                 out=w3_sc_raw[32 * q : 32 * q + 4].bitcast(I32),
                 in_=w3_scales[:, 4 * q : 4 * q + 4, :].rearrange("a r n -> r a n").bitcast(I32),
             )
-        load_table(1, T // 2, T)
-        load_table(2, 0, T)
+        load_table(2, half_t, T)
         w1_raw = {}
         for a in range(KA):
             w1_raw[(0, a)] = load_weight(w1, a * K_PASS, 0)
@@ -134,17 +132,17 @@ def tile_list_trampoline_phase_features_kernel(
                 out=v_sc[a][0:112, :].bitcast(I32),
                 in_=v_sc[0][4 * a : 4 * a + 112, :].bitcast(I32),
             )
+        nc.vector.tensor_copy(out=v_codes[1][:], in_=tab[1][:].indirect(offs_t[:]))
         nc.vector.tensor_copy(
             out=w3_sc[:].rearrange("p a (t m) -> p a m t", t=PACK),
             in_=w3_sc_raw[:].rearrange("p a (m t) -> p a m t", t=PACK),
         )
-        for a in range(1, KA):
-            nc.vector.tensor_copy(out=v_codes[a][:], in_=tab[a][:].indirect(offs_t[:]))
+        nc.vector.tensor_copy(out=v_codes[2][:], in_=tab[2][:].indirect(offs_t[:]))
 
         skip_banks = {}
         for jh in range(JH):
             for t in range(PACK):
-                skip_banks[(jh, t)] = psum.tile([P, BANK], F32, name="bank", tag="bank")
+                skip_banks[(jh, t)] = psum.tile([P, BANK], F32, name="bank", tag="bank%d" % (PACK * jh + t))
         for a in range(KA):
             for jh in range(JH):
                 js = slice(jh * BANK, (jh + 1) * BANK)
@@ -163,8 +161,23 @@ def tile_list_trampoline_phase_features_kernel(
                 nc.scalar.copy(out=g2[t][:, jh * BANK : (jh + 1) * BANK], in_=skip_banks[(jh, t)][:])
 
         w1_q = {}
-        for a in range(KA):
-            w1_q[(0, a)] = quantise_weight(round_weight("vector", w1_raw[(0, a)], 1), "w1_0%d" % a)
+        for a in range(KA - 1):
+            w1_q[(0, a)] = quantise_weight(round_weight("vector", w1_raw[(0, a)], rounded_tile("grouped", 1, 2)[:]), "w1_0%d" % a)
+        last_codes = keep.tile([P, BANK], U32, name="w1_last_codes", align_bytes=64)
+        last_sc = keep.tile([P, BANK], U8, name="w1_last_sc", align_bytes=64)
+        for u in range(2):
+            half = ring.tile([P, 2, P, PACK], BF16, name="half", tag="grouped", bufs=2, align_bytes=64)
+            nc.vector.tensor_copy(
+                out=half[:].rearrange("p t m j -> p m j t"),
+                in_=w1_raw[(0, KA - 1)][:].rearrange("p j (m t) -> p m j t", t=PACK)[:, :, :, 2 * u : 2 * u + 2],
+            )
+            cols = slice(2 * P * u, 2 * P * (u + 1))
+            nc.vector.quantize_mx(
+                out=last_codes[:, cols].bitcast(FP8X4),
+                scales=last_sc[:, cols],
+                in_=half[:].rearrange("p t m j -> p (t m j)"),
+            )
+        w1_q[(0, KA - 1)] = (last_codes, last_sc)
         for a in range(KA):
             w1_raw[(1, a)] = load_weight(w1, a * K_PASS, BANK)
         w2_raw = [load_weight(w2, b * K_PASS, 0) for b in range(HB)]
@@ -179,42 +192,54 @@ def tile_list_trampoline_phase_features_kernel(
 
         def arguments(b, jh):
             js = slice(jh * BANK, (jh + 1) * BANK)
-            x = ring.tile([P, PACK, BANK], F32, name="x", tag="x", bufs=2, align_bytes=64)
+            x = ring.tile([P, PACK, BANK], F32, name="x", tag="x%d" % jh, bufs=1, align_bytes=64)
             xs[(b, jh)] = x
+            first = PACK if (b, jh) == (1, 0) else 0
+            banks = [psum.tile([P, BANK], F32, name="bank", tag="bank%d" % (first + t)) for t in range(PACK)]
+
+            order = [0, 1, 2]
+
+            def one_pass(t, n):
+                a = order[n]
+                codes, scales = w1_q[(b, a)]
+                nc.tensor.matmul_mx(
+                    out=banks[t][:],
+                    lhsT=codes[:, P * t : P * (t + 1)].bitcast(FP8X4),
+                    lhsT_scale=scales[:, P * t : P * (t + 1)],
+                    rhs=v_codes[a][:, js].bitcast(FP8X4),
+                    rhs_scale=v_sc[a][:, js],
+                    start=(n == 0),
+                    stop=(n == KA - 1),
+                )
+
+            ahead = KA - 1 if (b, jh) == (0, 0) else 0
             for t in range(PACK):
-                bank = psum.tile([P, BANK], F32, name="bank", tag="bank")
-                for a in range(KA):
-                    codes, scales = w1_q[(b, a)]
-                    nc.tensor.matmul_mx(
-                        out=bank[:],
-                        lhsT=codes[:, P * t : P * (t + 1)].bitcast(FP8X4),
-                        lhsT_scale=scales[:, P * t : P * (t + 1)],
-                        rhs=v_codes[a][:, js].bitcast(FP8X4),
-                        rhs_scale=v_sc[a][:, js],
-                        start=(a == 0),
-                        stop=(a == KA - 1),
-                    )
-                nc.scalar.activation(out=x[:, t, :], in_=bank[:], func=ACT.Identity, bias=shift_t[:, b, t : t + 1])
-                if b == 0 and jh == 0 and t == 0:
-                    nc.gpsimd.tensor_copy(out=clock[:, 0:1], in_=x[:, 0, 0:1])
+                for n in range(ahead):
+                    one_pass(t, n)
+            for t in range(PACK):
+                for n in range(ahead, KA):
+                    one_pass(t, n)
+                nc.scalar.activation(out=x[:, t, :], in_=banks[t][:], func=ACT.Identity, bias=shift_t[:, b, t : t + 1])
 
         def wrap(b, jh):
             x = xs[(b, jh)]
             turns = ring.tile([P, PACK, BANK], I32, name="turns", tag="turns", bufs=1, align_bytes=64)
-            for u in range(2):
-                ts = slice(2 * u, 2 * u + 2)
+            parts = 2 if jh == 0 else 1
+            width = PACK // parts
+            for u in range(parts):
+                ts = slice(width * u, width * (u + 1))
                 nc.vector.tensor_scalar(
                     out=turns[:, ts, :], in0=x[:, ts, :], scalar1=1.0 / TWO_PI, scalar2=None, op0=ALU.mult
                 )
-            for u in range(2):
-                ts = slice(2 * u, 2 * u + 2)
+            for u in range(parts):
+                ts = slice(width * u, width * (u + 1))
                 nc.vector.scalar_tensor_tensor(
                     out=x[:, ts, :], in0=turns[:, ts, :], scalar=-TWO_PI, in1=x[:, ts, :], op0=ALU.mult, op1=ALU.add
                 )
 
         def sine(b, jh):
             x = xs[(b, jh)]
-            sines = ring.tile([P, BANK, PACK], F32, name="sines", tag="sines", bufs=2, align_bytes=64)
+            sines = ring.tile([P, BANK, PACK], F32, name="sines", tag="sines%d" % jh, bufs=1, align_bytes=64)
             sines_of[(b, jh)] = sines
             for u in range(2):
                 cs = slice(u * BANK // 8, (u + 1) * BANK // 8)
@@ -227,66 +252,77 @@ def tile_list_trampoline_phase_features_kernel(
         def quantise_h(b, jh):
             sines = sines_of[(b, jh)]
             hb = ring.tile([P, BANK, PACK], BF16, name="hb", tag="hb", bufs=2, align_bytes=64)
-            for u in range(2):
-                hs = slice(u * BANK // 2, (u + 1) * BANK // 2)
+            parts = 2 if (b, jh) == (1, 1) else 1
+            for u in range(parts):
+                hs = slice(u * BANK // parts, (u + 1) * BANK // parts)
                 nc.vector.tensor_tensor(
                     out=hb[:, hs, :],
                     in0=sines[:, hs, :],
-                    in1=gain_t[:, b, :].unsqueeze(1).to_broadcast([P, BANK // 2, PACK]),
+                    in1=gain_t[:, b, :].unsqueeze(1).to_broadcast([P, BANK // parts, PACK]),
                     op=ALU.mult,
                 )
             codes = keep.tile([P, BANK], U32, name="h_codes%d%d" % (b, jh), align_bytes=64)
             scales = keep.tile([P, BANK], U8, name="h_sc%d%d" % (b, jh), align_bytes=64)
             nc.vector.quantize_mx(out=codes[:].bitcast(FP8X4), scales=scales[:], in_=hb[:].rearrange("p j t -> p (j t)"))
             h_q[(b, jh)] = (codes, scales)
-            if b == 1 and jh == 0:
-                nc.gpsimd.tensor_copy(out=clock2[:, 0:1], in_=codes[:, 0:1])
 
-        def mix(jh):
+        mix_banks = {}
+
+        def mix_pass(b, jh):
             js = slice(jh * BANK, (jh + 1) * BANK)
             for t in range(PACK):
-                bank = psum.tile([P, BANK], F32, name="bank", tag="bank")
-                for b in range(HB):
-                    nc.tensor.matmul_mx(
-                        out=bank[:],
-                        lhsT=w2_q[b][0][:, P * t : P * (t + 1)].bitcast(FP8X4),
-                        lhsT_scale=w2_q[b][1][:, P * t : P * (t + 1)],
-                        rhs=h_q[(b, jh)][0][:].bitcast(FP8X4),
-                        rhs_scale=h_q[(b, jh)][1][:],
-                        start=(b == 0),
-                        stop=(b == HB - 1),
-                    )
-                nc.vector.tensor_tensor(out=g2[t][:, js], in0=bank[:], in1=g2[t][:, js], op=ALU.max)
+                if b == 0:
+                    mix_banks[(jh, t)] = psum.tile([P, BANK], F32, name="bank", tag="bank%d" % (PACK * (1 - jh) + t))
+                bank = mix_banks[(jh, t)]
+                nc.tensor.matmul_mx(
+                    out=bank[:],
+                    lhsT=w2_q[b][0][:, P * t : P * (t + 1)].bitcast(FP8X4),
+                    lhsT_scale=w2_q[b][1][:, P * t : P * (t + 1)],
+                    rhs=h_q[(b, jh)][0][:].bitcast(FP8X4),
+                    rhs_scale=h_q[(b, jh)][1][:],
+                    start=(b == 0),
+                    stop=(b == HB - 1),
+                )
 
-        def w1_piece(engine, a):
-            w1_q[(1, a)] = quantise_weight(round_weight(engine, w1_raw[(1, a)], 2), "w1_1%d" % a)
+        def larger(jh):
+            js = slice(jh * BANK, (jh + 1) * BANK)
+            for t in range(PACK):
+                nc.vector.tensor_tensor(out=g2[t][:, js], in0=mix_banks[(jh, t)][:], in1=g2[t][:, js], op=ALU.max)
 
-        def w2_piece(b):
-            w2_q.append(quantise_weight(round_weight("scalar", w2_raw[b], 2), "w2_%d" % b))
-
+        wide = PACK * BANK
         arguments(0, 0)
         wrap(0, 0)
         arguments(0, 1)
         sine(0, 0)
         wrap(0, 1)
-        w1_piece("scalar", 0)
+        two = rounded_tile("x0", 2, 1)
+        g10 = round_weight("scalar", w1_raw[(1, 0)], two[:, :wide])
+        g11 = round_weight("scalar", w1_raw[(1, 1)], two[:, wide:])
         quantise_h(0, 0)
         sine(0, 1)
-        w1_piece("scalar", 1)
-        w1_piece("vector", 2)
+        g12 = round_weight("vector", w1_raw[(1, 2)], rounded_tile("turns", 1, 1)[:])
+        w1_q[(1, 0)] = quantise_weight(g10, "w1_10")
+        w1_q[(1, 1)] = quantise_weight(g11, "w1_11")
+        w1_q[(1, 2)] = quantise_weight(g12, "w1_12")
+        g20 = round_weight("scalar", w2_raw[0], rounded_tile("x1", 1, 1)[:])
         arguments(1, 0)
         quantise_h(0, 1)
+        w2_q.append(quantise_weight(g20, "w2_0"))
         wrap(1, 0)
-        w2_piece(0)
         arguments(1, 1)
+        mix_pass(0, 0)
+        mix_pass(0, 1)
         sine(1, 0)
         wrap(1, 1)
-        w2_piece(1)
+        g21 = round_weight("scalar", w2_raw[1], rounded_tile("x0", 1, 1)[:])
         quantise_h(1, 0)
         sine(1, 1)
-        mix(0)
+        w2_q.append(quantise_weight(g21, "w2_1"))
+        mix_pass(1, 0)
         quantise_h(1, 1)
-        mix(1)
+        mix_pass(1, 1)
+        larger(0)
+        larger(1)
 
         y_codes = keep.tile([P, PAIRS], U32, name="y_codes", align_bytes=64)
         y_sc = keep.tile([P, PAIRS], U8, name="y_sc", align_bytes=64)

@@ -54,15 +54,12 @@ def tile_list_trampoline_phase_features_kernel(
         shift_t = keep.tile([P, HB, PACK], F32, name="shift_t")
         gain_t = keep.tile([P, HB, PACK], F32, name="gain_t")
         g2 = [keep.tile([P, S], F32, name="g2_%d" % t, align_bytes=64) for t in range(PACK)]
-        warm = keep.tile([P, 2], F32, name="warm")
 
         nc.gpsimd.memset(tab_sc[:, : T // 2].bitcast(I32), 0)
         nc.vector.memset(tab_sc[:, T // 2 :].bitcast(I32), 0)
         nc.vector.memset(w3_sc_raw[:].rearrange("p a n -> p (a n)").bitcast(I32), 0)
         for a in range(1, KA):
             nc.vector.memset(v_sc[a][:].bitcast(I32), 0)
-        nc.vector.memset(warm[:], 0.0)
-        nc.scalar.activation(out=warm[:, 1:2], in_=warm[:, 0:1], func=ACT.Sin)
 
         def load_table(a, c0, c1):
             words = tab_words[a].rearrange("p t i -> p (t i)").bitcast(I32)
@@ -187,20 +184,18 @@ def tile_list_trampoline_phase_features_kernel(
         h_q = {}
         w2_q = []
 
-        xs = {}
-        sines_of = {}
+        wrapped = {}
+        scaled = {}
+        woven = {}
 
         def arguments(b, jh):
             js = slice(jh * BANK, (jh + 1) * BANK)
             x = ring.tile([P, PACK, BANK], F32, name="x", tag="x%d" % jh, bufs=1, align_bytes=64)
-            xs[(b, jh)] = x
+            wrapped[(b, jh)] = x
             first = PACK if (b, jh) == (1, 0) else 0
             banks = [psum.tile([P, BANK], F32, name="bank", tag="bank%d" % (first + t)) for t in range(PACK)]
 
-            order = [0, 1, 2]
-
-            def one_pass(t, n):
-                a = order[n]
+            def one_pass(t, a):
                 codes, scales = w1_q[(b, a)]
                 nc.tensor.matmul_mx(
                     out=banks[t][:],
@@ -208,62 +203,73 @@ def tile_list_trampoline_phase_features_kernel(
                     lhsT_scale=scales[:, P * t : P * (t + 1)],
                     rhs=v_codes[a][:, js].bitcast(FP8X4),
                     rhs_scale=v_sc[a][:, js],
-                    start=(n == 0),
-                    stop=(n == KA - 1),
+                    start=(a == 0),
+                    stop=(a == KA - 1),
                 )
 
-            ahead = KA - 1 if (b, jh) == (0, 0) else 0
+            ahead = KA - 1 if jh == 0 else 0
             for t in range(PACK):
-                for n in range(ahead):
-                    one_pass(t, n)
-            for t in range(PACK):
-                for n in range(ahead, KA):
-                    one_pass(t, n)
-                nc.scalar.activation(out=x[:, t, :], in_=banks[t][:], func=ACT.Identity, bias=shift_t[:, b, t : t + 1])
-
-        def wrap(b, jh):
-            x = xs[(b, jh)]
-            turns = ring.tile([P, PACK, BANK], I32, name="turns", tag="turns", bufs=1, align_bytes=64)
-            parts = 2 if jh == 0 else 1
-            width = PACK // parts
-            for u in range(parts):
-                ts = slice(width * u, width * (u + 1))
-                nc.vector.tensor_scalar(
-                    out=turns[:, ts, :], in0=x[:, ts, :], scalar1=1.0 / TWO_PI, scalar2=None, op0=ALU.mult
-                )
-            for u in range(parts):
-                ts = slice(width * u, width * (u + 1))
-                nc.vector.scalar_tensor_tensor(
-                    out=x[:, ts, :], in0=turns[:, ts, :], scalar=-TWO_PI, in1=x[:, ts, :], op0=ALU.mult, op1=ALU.add
-                )
+                for a in range(ahead):
+                    one_pass(t, a)
+            for u in range(2):
+                turns = {}
+                for t in range(2 * u, 2 * u + 2):
+                    for a in range(ahead, KA):
+                        one_pass(t, a)
+                    turns[t] = ring.tile([P, BANK], I32, name="turns", tag="turns", bufs=2, align_bytes=64)
+                    nc.vector.tensor_scalar(
+                        out=turns[t][:],
+                        in0=banks[t][:],
+                        scalar1=shift_t[:, b, t : t + 1],
+                        scalar2=1.0 / TWO_PI,
+                        op0=ALU.add,
+                        op1=ALU.mult,
+                    )
+                for t in range(2 * u, 2 * u + 2):
+                    nc.vector.scalar_tensor_tensor(
+                        out=x[:, t, :], in0=turns[t][:], scalar=-TWO_PI, in1=banks[t][:], op0=ALU.mult, op1=ALU.add
+                    )
 
         def sine(b, jh):
-            x = xs[(b, jh)]
-            sines = ring.tile([P, BANK, PACK], F32, name="sines", tag="sines%d" % jh, bufs=1, align_bytes=64)
-            sines_of[(b, jh)] = sines
-            for u in range(2):
-                cs = slice(u * BANK // 8, (u + 1) * BANK // 8)
-                nc.scalar.activation(
-                    out=sines[:].rearrange("p (c i) t -> p c t i", i=4)[:, cs],
-                    in_=x[:].rearrange("p t (c i) -> p c t i", i=4)[:, cs],
-                    func=ACT.Sin,
+            x = wrapped[(b, jh)]
+            hg = ring.tile([P, PACK, BANK], BF16, name="hg", tag="hg", bufs=2, align_bytes=64)
+            scaled[(b, jh)] = hg
+            for t in range(PACK):
+                sines = ring.tile([P, BANK], F32, name="sines", tag="sines", bufs=4, align_bytes=64)
+                nc.scalar.activation(out=sines[:], in_=x[:, t, :], func=ACT.Sin, bias=shift_t[:, b, t : t + 1])
+                nc.gpsimd.tensor_scalar(
+                    out=hg[:, t, :], in0=sines[:], scalar1=gain_t[:, b, t : t + 1], scalar2=0.0, op0=ALU.mult, op1=ALU.add
                 )
 
-        def quantise_h(b, jh):
-            sines = sines_of[(b, jh)]
+        def weave(b, jh, engine):
+            hg = scaled[(b, jh)]
             hb = ring.tile([P, BANK, PACK], BF16, name="hb", tag="hb", bufs=2, align_bytes=64)
-            parts = 2 if (b, jh) == (1, 1) else 1
-            for u in range(parts):
-                hs = slice(u * BANK // parts, (u + 1) * BANK // parts)
-                nc.vector.tensor_tensor(
-                    out=hb[:, hs, :],
-                    in0=sines[:, hs, :],
-                    in1=gain_t[:, b, :].unsqueeze(1).to_broadcast([P, BANK // parts, PACK]),
-                    op=ALU.mult,
-                )
+            woven[(b, jh)] = hb
+            if engine == "gpsimd":
+                for u in range(4):
+                    cs = slice(u * BANK // 4, (u + 1) * BANK // 4)
+                    nc.gpsimd.tensor_scalar(
+                        out=hb[:, cs, :],
+                        in0=hg[:].rearrange("p t j -> p j t")[:, cs, :],
+                        scalar1=1.0,
+                        scalar2=0.0,
+                        op0=ALU.mult,
+                        op1=ALU.add,
+                    )
+            else:
+                dst = hb[:].rearrange("p (c i) t -> p c t i", i=4)
+                src = hg[:].rearrange("p t (c i) -> p c t i", i=4)
+                if engine == "vector":
+                    nc.vector.tensor_copy(out=dst, in_=src)
+                else:
+                    nc.scalar.copy(out=dst, in_=src)
+
+        def quantise_h(b, jh):
             codes = keep.tile([P, BANK], U32, name="h_codes%d%d" % (b, jh), align_bytes=64)
             scales = keep.tile([P, BANK], U8, name="h_sc%d%d" % (b, jh), align_bytes=64)
-            nc.vector.quantize_mx(out=codes[:].bitcast(FP8X4), scales=scales[:], in_=hb[:].rearrange("p j t -> p (j t)"))
+            nc.vector.quantize_mx(
+                out=codes[:].bitcast(FP8X4), scales=scales[:], in_=woven[(b, jh)][:].rearrange("p j t -> p (j t)")
+            )
             h_q[(b, jh)] = (codes, scales)
 
         mix_banks = {}
@@ -291,34 +297,34 @@ def tile_list_trampoline_phase_features_kernel(
 
         wide = PACK * BANK
         arguments(0, 0)
-        wrap(0, 0)
-        arguments(0, 1)
         sine(0, 0)
-        wrap(0, 1)
+        g10 = round_weight("scalar", w1_raw[(1, 0)], rounded_tile("grouped", 1, 2)[:])
         two = rounded_tile("x0", 2, 1)
-        g10 = round_weight("scalar", w1_raw[(1, 0)], two[:, :wide])
-        g11 = round_weight("scalar", w1_raw[(1, 1)], two[:, wide:])
-        quantise_h(0, 0)
-        sine(0, 1)
-        g12 = round_weight("vector", w1_raw[(1, 2)], rounded_tile("turns", 1, 1)[:])
+        g11 = round_weight("scalar", w1_raw[(1, 1)], two[:, :wide])
+        g12 = round_weight("scalar", w1_raw[(1, 2)], two[:, wide:])
+        weave(0, 0, "gpsimd")
+        arguments(0, 1)
         w1_q[(1, 0)] = quantise_weight(g10, "w1_10")
         w1_q[(1, 1)] = quantise_weight(g11, "w1_11")
         w1_q[(1, 2)] = quantise_weight(g12, "w1_12")
+        sine(0, 1)
+        quantise_h(0, 0)
+        weave(0, 1, "gpsimd")
         g20 = round_weight("scalar", w2_raw[0], rounded_tile("x1", 1, 1)[:])
-        arguments(1, 0)
-        quantise_h(0, 1)
         w2_q.append(quantise_weight(g20, "w2_0"))
-        wrap(1, 0)
+        arguments(1, 0)
+        sine(1, 0)
+        quantise_h(0, 1)
+        g21 = round_weight("scalar", w2_raw[1], rounded_tile("x0", 1, 1)[:])
         arguments(1, 1)
         mix_pass(0, 0)
-        mix_pass(0, 1)
-        sine(1, 0)
-        wrap(1, 1)
-        g21 = round_weight("scalar", w2_raw[1], rounded_tile("x0", 1, 1)[:])
-        quantise_h(1, 0)
         sine(1, 1)
+        weave(1, 0, "scalar")
         w2_q.append(quantise_weight(g21, "w2_1"))
+        quantise_h(1, 0)
+        mix_pass(0, 1)
         mix_pass(1, 0)
+        weave(1, 1, "vector")
         quantise_h(1, 1)
         mix_pass(1, 1)
         larger(0)

@@ -55,9 +55,9 @@ def tile_list_trampoline_phase_features_kernel(
         gain_t = keep.tile([P, HB, PACK], F32, name="gain_t")
         g2 = [keep.tile([P, S], F32, name="g2_%d" % t, align_bytes=64) for t in range(PACK)]
 
+        nc.gpsimd.memset(w3_sc_raw[:].rearrange("p a n -> p (a n)").bitcast(I32), 0)
         nc.gpsimd.memset(tab_sc[:, : T // 2].bitcast(I32), 0)
         nc.vector.memset(tab_sc[:, T // 2 :].bitcast(I32), 0)
-        nc.vector.memset(w3_sc_raw[:].rearrange("p a n -> p (a n)").bitcast(I32), 0)
         for a in range(1, KA):
             nc.vector.memset(v_sc[a][:].bitcast(I32), 0)
 
@@ -91,37 +91,41 @@ def tile_list_trampoline_phase_features_kernel(
             return codes, scales
 
         half_t = T // 2
-        load_table(0, 0, half_t)
+        quarter = T // 4
+        load_table(0, 0, quarter)
         nc.sync.dma_start(offs_t[:], offs)
         nc.sync.dma_start(out=w3_raw[:].bitcast(I32), in_=w3_words.rearrange("a p c -> p a c").bitcast(I32))
-        nc.sync.dma_start(out=shift_t[:], in_=shift.rearrange("(b p t) -> p b t", p=P, t=PACK))
-        nc.sync.dma_start(out=gain_t[:], in_=gain.rearrange("(b p t) -> p b t", p=P, t=PACK))
-        load_table(0, half_t, T)
-        nc.sync.dma_start(pos1_t[:], pos1)
-        nc.sync.dma_start(pos2_t[:], pos2)
-        load_table(1, 0, half_t)
-        for q in range(4):
-            nc.sync.dma_start(
-                out=tab_sc[32 * q : 32 * q + 4 * KA, :].bitcast(I32),
-                in_=tab_scales[:, 4 * q : 4 * q + 4, :].bitcast(I32),
-            )
-        load_table(1, half_t, T)
-        load_table(2, 0, half_t)
+        load_table(0, quarter, 2 * quarter)
         for q in range(4):
             nc.sync.dma_start(
                 out=w3_sc_raw[32 * q : 32 * q + 4].bitcast(I32),
                 in_=w3_scales[:, 4 * q : 4 * q + 4, :].rearrange("a r n -> r a n").bitcast(I32),
             )
-        load_table(2, half_t, T)
+        load_table(0, 2 * quarter, 3 * quarter)
+        load_table(0, 3 * quarter, T)
+        for q in range(4):
+            nc.sync.dma_start(
+                out=tab_sc[32 * q : 32 * q + 4 * KA, :].bitcast(I32),
+                in_=tab_scales[:, 4 * q : 4 * q + 4, :].bitcast(I32),
+            )
+        for a in range(1, KA):
+            load_table(a, 0, half_t)
+            load_table(a, half_t, T)
+        nc.sync.dma_start(out=shift_t[:], in_=shift.rearrange("(b p t) -> p b t", p=P, t=PACK))
         w1_raw = {}
         for a in range(KA):
             w1_raw[(0, a)] = load_weight(w1, a * K_PASS, 0)
+        nc.sync.dma_start(out=gain_t[:], in_=gain.rearrange("(b p t) -> p b t", p=P, t=PACK))
 
         for a in range(KA):
             nc.vector.tensor_copy(
                 out=w3_codes[:, a, :].rearrange("p (t m b) -> p m t b", t=PACK, b=2),
                 in_=w3_raw[:, a, :].rearrange("p (m t b) -> p m t b", t=PACK, b=2),
             )
+        nc.vector.tensor_copy(
+            out=w3_sc[:].rearrange("p a (t m) -> p a m t", t=PACK),
+            in_=w3_sc_raw[:].rearrange("p a (m t) -> p a m t", t=PACK),
+        )
         nc.vector.tensor_copy(out=v_codes[0][:], in_=tab[0][:].indirect(offs_t[:]))
         nc.vector.tensor_copy(out=v_sc[0][:], in_=tab_sc[:].indirect(offs_t[:]))
         for a in range(1, KA):
@@ -130,10 +134,6 @@ def tile_list_trampoline_phase_features_kernel(
                 in_=v_sc[0][4 * a : 4 * a + 112, :].bitcast(I32),
             )
         nc.vector.tensor_copy(out=v_codes[1][:], in_=tab[1][:].indirect(offs_t[:]))
-        nc.vector.tensor_copy(
-            out=w3_sc[:].rearrange("p a (t m) -> p a m t", t=PACK),
-            in_=w3_sc_raw[:].rearrange("p a (m t) -> p a m t", t=PACK),
-        )
         nc.vector.tensor_copy(out=v_codes[2][:], in_=tab[2][:].indirect(offs_t[:]))
 
         skip_banks = {}
@@ -179,6 +179,8 @@ def tile_list_trampoline_phase_features_kernel(
             w1_raw[(1, a)] = load_weight(w1, a * K_PASS, BANK)
         w2_raw = [load_weight(w2, b * K_PASS, 0) for b in range(HB)]
         emph_t = ring.tile([P, PACK, PAIRS], F32, name="emph_t", tag="raw", bufs=4, align_bytes=64)
+        nc.sync.dma_start(pos1_t[:], pos1)
+        nc.sync.dma_start(pos2_t[:], pos2)
         nc.sync.dma_start(out=emph_t[:], in_=emph.rearrange("(p t) m -> p t m", t=PACK))
 
         h_q = {}
@@ -208,8 +210,8 @@ def tile_list_trampoline_phase_features_kernel(
                 )
 
             ahead = KA - 1 if jh == 0 else 0
-            for t in range(PACK):
-                for a in range(ahead):
+            for a in range(ahead):
+                for t in range(PACK):
                     one_pass(t, a)
             for u in range(2):
                 turns = {}
@@ -334,38 +336,40 @@ def tile_list_trampoline_phase_features_kernel(
         y_sc = keep.tile([P, PAIRS], U8, name="y_sc", align_bytes=64)
         out_rows = out_0.rearrange("(p t) m -> p t m", t=PACK)
         out_words = out_1[0].rearrange("p m t -> p (m t)").bitcast(I32)
+        y = ring.tile([P, PACK, PAIRS], F32, name="y", tag="x1", bufs=1, align_bytes=64)
+        for u in range(2):
+            first = []
+            both = []
+            for t in range(2 * u, 2 * u + 2):
+                take = ring.tile([P, PAIRS], F32, name="take", tag="take", bufs=2, align_bytes=64)
+                nc.vector.tensor_copy(out=take[:], in_=g2[t][:].indirect(pos1_t[:]))
+                first.append(take)
+            for t in range(2 * u, 2 * u + 2):
+                pair = ring.tile([P, PAIRS], F32, name="pair", tag="pair", bufs=2, align_bytes=64)
+                nc.vector.tensor_tensor(out=pair[:], in0=g2[t][:].indirect(pos2_t[:]), in1=first[t - 2 * u][:], op=ALU.add)
+                both.append(pair)
+            for t in range(2 * u, 2 * u + 2):
+                nc.vector.tensor_tensor(out=y[:, t, :], in0=both[t - 2 * u][:], in1=emph_t[:, t, :], op=ALU.mult)
+                nc.sync.dma_start(out=out_rows[:, t, :], in_=y[:, t, :])
+        rounded = []
         for mh in range(MH):
             ms = slice(mh * MW, (mh + 1) * MW)
-            ls = slice(mh * MW // 16, (mh + 1) * MW // 16)
-            y = ring.tile([P, PACK, MW], F32, name="y", tag="y", bufs=2, align_bytes=64)
-            for u in range(2):
-                first = []
-                both = []
-                for t in range(2 * u, 2 * u + 2):
-                    take = ring.tile([P, MW], F32, name="take", tag="take", bufs=2, align_bytes=64)
-                    nc.vector.tensor_copy(out=take[:], in_=g2[t][:].indirect(pos1_t[:, ls]))
-                    first.append(take)
-                for t in range(2 * u, 2 * u + 2):
-                    pair = ring.tile([P, MW], F32, name="pair", tag="pair", bufs=2, align_bytes=64)
-                    nc.vector.tensor_tensor(
-                        out=pair[:], in0=g2[t][:].indirect(pos2_t[:, ls]), in1=first[t - 2 * u][:], op=ALU.add
-                    )
-                    both.append(pair)
-                for t in range(2 * u, 2 * u + 2):
-                    nc.vector.tensor_tensor(out=y[:, t, :], in0=both[t - 2 * u][:], in1=emph_t[:, t, ms], op=ALU.mult)
-                nc.sync.dma_start(out=out_rows[:, 2 * u : 2 * u + 2, ms], in_=y[:, 2 * u : 2 * u + 2, :])
             yb = ring.tile([P, MW, PACK], BF16, name="yb", tag="hb", bufs=2, align_bytes=64)
             dst = yb[:].rearrange("p (c i) t -> p c t i", i=4)
-            src = y[:].rearrange("p t (c i) -> p c t i", i=4)
-            if mh == MH - 1:
+            src = y[:, :, ms].rearrange("p t (c i) -> p c t i", i=4)
+            if mh == 0:
                 nc.vector.tensor_copy(out=dst, in_=src)
             else:
                 nc.scalar.copy(out=dst, in_=src)
+            rounded.append(yb)
+        for mh in range(MH):
+            ms = slice(mh * MW, (mh + 1) * MW)
             nc.vector.quantize_mx(
-                out=y_codes[:, ms].bitcast(FP8X4), scales=y_sc[:, ms], in_=yb[:].rearrange("p m t -> p (m t)")
+                out=y_codes[:, ms].bitcast(FP8X4), scales=y_sc[:, ms], in_=rounded[mh][:].rearrange("p m t -> p (m t)")
             )
             nc.sync.dma_start(out=out_words[:, ms], in_=y_codes[:, ms].bitcast(I32))
         for q in range(4):
-            nc.scalar.dma_start(
+            queue = nc.scalar if q % 2 == 0 else nc.sync
+            queue.dma_start(
                 out=out_2[0, 4 * q : 4 * q + 4, :].bitcast(I32), in_=y_sc[32 * q : 32 * q + 4, :].bitcast(I32)
             )

import math
from contextlib import ExitStack

import concourse.mybir as mybir

K, H, N, T, S, PAIRS = 1536, 1024, 512, 4096, 1024, 512
FLOPS = 2 * K * H * S + 2 * H * N * S + 2 * K * N * S

F32 = mybir.dt.float32
BF16 = mybir.dt.bfloat16
I32 = mybir.dt.int32
U32 = mybir.dt.uint32
U16 = mybir.dt.uint16
U8 = mybir.dt.uint8
FP8X4 = mybir.dt.float8_e4m3fn_x4
FP4X4 = mybir.dt.float4_e2m1fn_x4
ALU = mybir.AluOpType
ACT = mybir.ActivationFunctionType

P = 128
PACK = 4
K_PASS = P * PACK
BANK = 512
KA = K // K_PASS
HB = H // K_PASS
JH = S // BANK
MH = 2
MW = PAIRS // MH
TWO_PI = 2.0 * math.pi


def tile_list_trampoline_phase_features_kernel(
    tc, tab_words, tab_scales, offs, pos1, pos2, w1, shift, gain, w2, w3_words, w3_scales, emph, out_0, out_1, out_2
):
    nc = tc.nc
    with ExitStack() as ctx:
        lists = ctx.enter_context(tc.tile_pool(name="lists", bufs=1))
        keep = ctx.enter_context(tc.tile_pool(name="keep", bufs=1))
        ring = ctx.enter_context(tc.tile_pool(name="ring", bufs=2))
        psum = ctx.enter_context(tc.psum_pool(name="psum", bufs=1))

        offs_t = lists.tile([P, S // 16], U16, name="offs_t")
        pos1_t = lists.tile([P, PAIRS // 16], U16, name="pos1_t")
        pos2_t = lists.tile([P, PAIRS // 16], U16, name="pos2_t")

        tab = [keep.tile([P, T], U32, name="tab%d" % a, align_bytes=64) for a in range(KA)]
        tab_sc = keep.tile([P, T], U8, name="tab_sc", align_bytes=64)
        v_codes = [keep.tile([P, S], U32, name="v_codes%d" % a, align_bytes=64) for a in range(KA)]
        v_sc = [keep.tile([P, S], U8, name="v_sc%d" % a, align_bytes=64) for a in range(KA)]
        w3_raw = keep.tile([P, KA, 2 * N], U8, name="w3_raw", align_bytes=64)
        w3_sc_raw = keep.tile([P, KA, N], U8, name="w3_sc_raw", align_bytes=64)
        w3_codes = keep.tile([P, KA, 2 * N], U8, name="w3_codes", align_bytes=64)
        w3_sc = keep.tile([P, KA, N], U8, name="w3_sc", align_bytes=64)
        shift_t = keep.tile([P, HB, PACK], F32, name="shift_t")
        gain_t = keep.tile([P, HB, PACK], F32, name="gain_t")
        g2 = [keep.tile([P, S], F32, name="g2_%d" % t, align_bytes=64) for t in range(PACK)]

        nc.gpsimd.memset(w3_sc_raw[:].rearrange("p a n -> p (a n)").bitcast(I32), 0)
        nc.gpsimd.memset(tab_sc[:, : T // 2].bitcast(I32), 0)
        nc.vector.memset(tab_sc[:, T // 2 :].bitcast(I32), 0)
        for a in range(1, KA):
            nc.vector.memset(v_sc[a][:].bitcast(I32), 0)

        def load_table(a, c0, c1):
            words = tab_words[a].rearrange("p t i -> p (t i)").bitcast(I32)
            nc.sync.dma_start(out=tab[a][:, c0:c1].bitcast(I32), in_=words[:, c0:c1])

        def load_weight(w, k0, c0):
            raw = ring.tile([P, PACK, BANK], F32, name="raw", tag="raw", bufs=4, align_bytes=64)
            nc.sync.dma_start(
                out=raw[:], in_=w[k0 : k0 + K_PASS, c0 : c0 + BANK].rearrange("(p j) c -> p j c", j=PACK)
            )
            return raw

        def round_weight(engine, raw, grouped):
            src = raw[:].rearrange("p j (m t) -> p m j t", t=PACK)
            dst = grouped.rearrange("p (t m j) -> p m j t", t=PACK, j=PACK)
            if engine == "vector":
                nc.vector.tensor_copy(out=dst, in_=src)
            else:
                nc.scalar.copy(out=dst, in_=src)
            return grouped

        def rounded_tile(tag, pieces, bufs):
            return ring.tile([P, pieces * PACK * BANK], BF16, name="grouped", tag=tag, bufs=bufs, align_bytes=64)

        def quantise_weight(grouped, name):
            codes = keep.tile([P, BANK], U32, name=name + "_codes", align_bytes=64)
            scales = keep.tile([P, BANK], U8, name=name + "_sc", align_bytes=64)
            nc.vector.quantize_mx(out=codes[:].bitcast(FP8X4), scales=scales[:], in_=grouped)
            return codes, scales

        half_t = T // 2
        quarter = T // 4
        load_table(0, 0, quarter)
        nc.sync.dma_start(offs_t[:], offs)
        nc.sync.dma_start(out=w3_raw[:].bitcast(I32), in_=w3_words.rearrange("a p c -> p a c").bitcast(I32))
        load_table(0, quarter, 2 * quarter)
        for q in range(4):
            nc.sync.dma_start(
                out=w3_sc_raw[32 * q : 32 * q + 4].bitcast(I32),
                in_=w3_scales[:, 4 * q : 4 * q + 4, :].rearrange("a r n -> r a n").bitcast(I32),
            )
        load_table(0, 2 * quarter, 3 * quarter)
        load_table(0, 3 * quarter, T)
        for q in range(4):
            nc.sync.dma_start(
                out=tab_sc[32 * q : 32 * q + 4 * KA, :].bitcast(I32),
                in_=tab_scales[:, 4 * q : 4 * q + 4, :].bitcast(I32),
            )
        for a in range(1, KA):
            load_table(a, 0, half_t)
            load_table(a, half_t, T)
        nc.sync.dma_start(out=shift_t[:], in_=shift.rearrange("(b p t) -> p b t", p=P, t=PACK))
        w1_raw = {}
        for a in range(KA):
            w1_raw[(0, a)] = load_weight(w1, a * K_PASS, 0)
        nc.sync.dma_start(out=gain_t[:], in_=gain.rearrange("(b p t) -> p b t", p=P, t=PACK))

        for a in range(KA):
            nc.vector.tensor_copy(
                out=w3_codes[:, a, :].rearrange("p (t m b) -> p m t b", t=PACK, b=2),
                in_=w3_raw[:, a, :].rearrange("p (m t b) -> p m t b", t=PACK, b=2),
            )
        nc.vector.tensor_copy(
            out=w3_sc[:].rearrange("p a (t m) -> p a m t", t=PACK),
            in_=w3_sc_raw[:].rearrange("p a (m t) -> p a m t", t=PACK),
        )
        nc.vector.tensor_copy(out=v_codes[0][:], in_=tab[0][:].indirect(offs_t[:]))
        nc.vector.tensor_copy(out=v_sc[0][:], in_=tab_sc[:].indirect(offs_t[:]))
        for a in range(1, KA):
            nc.scalar.dma_start(
                out=v_sc[a][0:112, :].bitcast(I32),
                in_=v_sc[0][4 * a : 4 * a + 112, :].bitcast(I32),
            )
        nc.vector.tensor_copy(out=v_codes[1][:], in_=tab[1][:].indirect(offs_t[:]))
        nc.vector.tensor_copy(out=v_codes[2][:], in_=tab[2][:].indirect(offs_t[:]))

        skip_banks = {}
        for jh in range(JH):
            for t in range(PACK):
                skip_banks[(jh, t)] = psum.tile([P, BANK], F32, name="bank", tag="bank%d" % (PACK * jh + t))
        for a in range(KA):
            for jh in range(JH):
                js = slice(jh * BANK, (jh + 1) * BANK)
                for t in range(PACK):
                    nc.tensor.matmul_mx(
                        out=skip_banks[(jh, t)][:],
                        lhsT=w3_codes[:, a, 2 * P * t : 2 * P * (t + 1)].bitcast(FP4X4),
                        lhsT_scale=w3_sc[:, a, P * t : P * (t + 1)],
                        rhs=v_codes[a][:, js].bitcast(FP8X4),
                        rhs_scale=v_sc[a][:, js],
                        start=(a == 0),
                        stop=(a == KA - 1),
                    )
        for jh in range(JH):
            for t in range(PACK):
                nc.scalar.copy(out=g2[t][:, jh * BANK : (jh + 1) * BANK], in_=skip_banks[(jh, t)][:])

        w1_q = {}
        for a in range(KA - 1):
            w1_q[(0, a)] = quantise_weight(round_weight("vector", w1_raw[(0, a)], rounded_tile("grouped", 1, 2)[:]), "w1_0%d" % a)
        last_codes = keep.tile([P, BANK], U32, name="w1_last_codes", align_bytes=64)
        last_sc = keep.tile([P, BANK], U8, name="w1_last_sc", align_bytes=64)
        for u in range(2):
            half = ring.tile([P, 2, P, PACK], BF16, name="half", tag="grouped", bufs=2, align_bytes=64)
            nc.vector.tensor_copy(
                out=half[:].rearrange("p t m j -> p m j t"),
                in_=w1_raw[(0, KA - 1)][:].rearrange("p j (m t) -> p m j t", t=PACK)[:, :, :, 2 * u : 2 * u + 2],
            )
            cols = slice(2 * P * u, 2 * P * (u + 1))
            nc.vector.quantize_mx(
                out=last_codes[:, cols].bitcast(FP8X4),
                scales=last_sc[:, cols],
                in_=half[:].rearrange("p t m j -> p (t m j)"),
            )
        w1_q[(0, KA - 1)] = (last_codes, last_sc)
        for a in range(KA):
            w1_raw[(1, a)] = load_weight(w1, a * K_PASS, BANK)
        w2_raw = [load_weight(w2, b * K_PASS, 0) for b in range(HB)]
        emph_t = ring.tile([P, PACK, PAIRS], F32, name="emph_t", tag="raw", bufs=4, align_bytes=64)
        nc.sync.dma_start(pos1_t[:], pos1)
        nc.sync.dma_start(pos2_t[:], pos2)
        nc.sync.dma_start(out=emph_t[:], in_=emph.rearrange("(p t) m -> p t m", t=PACK))

        h_q = {}
        w2_q = []

        wrapped = {}
        scaled = {}
        woven = {}

        def arguments(b, jh):
            js = slice(jh * BANK, (jh + 1) * BANK)
            x = ring.tile([P, PACK, BANK], F32, name="x", tag="x%d" % jh, bufs=1, align_bytes=64)
            wrapped[(b, jh)] = x
            first = PACK if (b, jh) == (1, 0) else 0
            banks = [psum.tile([P, BANK], F32, name="bank", tag="bank%d" % (first + t)) for t in range(PACK)]

            def one_pass(t, a):
                codes, scales = w1_q[(b, a)]
                nc.tensor.matmul_mx(
                    out=banks[t][:],
                    lhsT=codes[:, P * t : P * (t + 1)].bitcast(FP8X4),
                    lhsT_scale=scales[:, P * t : P * (t + 1)],
                    rhs=v_codes[a][:, js].bitcast(FP8X4),
                    rhs_scale=v_sc[a][:, js],
                    start=(a == 0),
                    stop=(a == KA - 1),
                )

            ahead = KA - 1 if jh == 0 else 0
            for a in range(ahead):
                for t in range(PACK):
                    one_pass(t, a)
            for u in range(2):
                turns = {}
                for t in range(2 * u, 2 * u + 2):
                    for a in range(ahead, KA):
                        one_pass(t, a)
                    turns[t] = ring.tile([P, BANK], I32, name="turns", tag="turns", bufs=2, align_bytes=64)
                    nc.vector.tensor_scalar(
                        out=turns[t][:],
                        in0=banks[t][:],
                        scalar1=shift_t[:, b, t : t + 1],
                        scalar2=1.0 / TWO_PI,
                        op0=ALU.add,
                        op1=ALU.mult,
                    )
                for t in range(2 * u, 2 * u + 2):
                    nc.vector.scalar_tensor_tensor(
                        out=x[:, t, :], in0=turns[t][:], scalar=-TWO_PI, in1=banks[t][:], op0=ALU.mult, op1=ALU.add
                    )

        def sine(b, jh):
            x = wrapped[(b, jh)]
            hg = ring.tile([P, PACK, BANK], BF16, name="hg", tag="hg", bufs=2, align_bytes=64)
            scaled[(b, jh)] = hg
            for t in range(PACK):
                sines = ring.tile([P, BANK], F32, name="sines", tag="sines", bufs=4, align_bytes=64)
                nc.scalar.activation(out=sines[:], in_=x[:, t, :], func=ACT.Sin, bias=shift_t[:, b, t : t + 1])
                nc.gpsimd.tensor_scalar(
                    out=hg[:, t, :], in0=sines[:], scalar1=gain_t[:, b, t : t + 1], scalar2=0.0, op0=ALU.mult, op1=ALU.add
                )

        def weave(b, jh, engine):
            hg = scaled[(b, jh)]
            hb = ring.tile([P, BANK, PACK], BF16, name="hb", tag="hb", bufs=2, align_bytes=64)
            woven[(b, jh)] = hb
            if engine == "gpsimd":
                for u in range(4):
                    cs = slice(u * BANK // 4, (u + 1) * BANK // 4)
                    nc.gpsimd.tensor_scalar(
                        out=hb[:, cs, :],
                        in0=hg[:].rearrange("p t j -> p j t")[:, cs, :],
                        scalar1=1.0,
                        scalar2=0.0,
                        op0=ALU.mult,
                        op1=ALU.add,
                    )
            else:
                dst = hb[:].rearrange("p (c i) t -> p c t i", i=4)
                src = hg[:].rearrange("p t (c i) -> p c t i", i=4)
                if engine == "vector":
                    nc.vector.tensor_copy(out=dst, in_=src)
                else:
                    nc.scalar.copy(out=dst, in_=src)

        def quantise_h(b, jh):
            codes = keep.tile([P, BANK], U32, name="h_codes%d%d" % (b, jh), align_bytes=64)
            scales = keep.tile([P, BANK], U8, name="h_sc%d%d" % (b, jh), align_bytes=64)
            nc.vector.quantize_mx(
                out=codes[:].bitcast(FP8X4), scales=scales[:], in_=woven[(b, jh)][:].rearrange("p j t -> p (j t)")
            )
            h_q[(b, jh)] = (codes, scales)

        mix_banks = {}

        def mix_pass(b, jh):
            js = slice(jh * BANK, (jh + 1) * BANK)
            for t in range(PACK):
                if b == 0:
                    mix_banks[(jh, t)] = psum.tile([P, BANK], F32, name="bank", tag="bank%d" % (PACK * (1 - jh) + t))
                bank = mix_banks[(jh, t)]
                nc.tensor.matmul_mx(
                    out=bank[:],
                    lhsT=w2_q[b][0][:, P * t : P * (t + 1)].bitcast(FP8X4),
                    lhsT_scale=w2_q[b][1][:, P * t : P * (t + 1)],
                    rhs=h_q[(b, jh)][0][:].bitcast(FP8X4),
                    rhs_scale=h_q[(b, jh)][1][:],
                    start=(b == 0),
                    stop=(b == HB - 1),
                )

        def larger(jh):
            js = slice(jh * BANK, (jh + 1) * BANK)
            for t in range(PACK):
                nc.vector.tensor_tensor(out=g2[t][:, js], in0=mix_banks[(jh, t)][:], in1=g2[t][:, js], op=ALU.max)

        wide = PACK * BANK
        arguments(0, 0)
        sine(0, 0)
        g10 = round_weight("scalar", w1_raw[(1, 0)], rounded_tile("grouped", 1, 2)[:])
        two = rounded_tile("x0", 2, 1)
        g11 = round_weight("scalar", w1_raw[(1, 1)], two[:, :wide])
        g12 = round_weight("scalar", w1_raw[(1, 2)], two[:, wide:])
        weave(0, 0, "gpsimd")
        arguments(0, 1)
        w1_q[(1, 0)] = quantise_weight(g10, "w1_10")
        w1_q[(1, 1)] = quantise_weight(g11, "w1_11")
        w1_q[(1, 2)] = quantise_weight(g12, "w1_12")
        sine(0, 1)
        quantise_h(0, 0)
        weave(0, 1, "gpsimd")
        g20 = round_weight("scalar", w2_raw[0], rounded_tile("x1", 1, 1)[:])
        w2_q.append(quantise_weight(g20, "w2_0"))
        arguments(1, 0)
        sine(1, 0)
        quantise_h(0, 1)
        g21 = round_weight("scalar", w2_raw[1], rounded_tile("x0", 1, 1)[:])
        arguments(1, 1)
        mix_pass(0, 0)
        sine(1, 1)
        weave(1, 0, "scalar")
        w2_q.append(quantise_weight(g21, "w2_1"))
        quantise_h(1, 0)
        mix_pass(0, 1)
        mix_pass(1, 0)
        weave(1, 1, "vector")
        quantise_h(1, 1)
        mix_pass(1, 1)
        larger(0)
        larger(1)

        y_codes = keep.tile([P, PAIRS], U32, name="y_codes", align_bytes=64)
        y_sc = keep.tile([P, PAIRS], U8, name="y_sc", align_bytes=64)
        out_rows = out_0.rearrange("(p t) m -> p t m", t=PACK)
        out_words = out_1[0].rearrange("p m t -> p (m t)").bitcast(I32)
        y = ring.tile([P, PACK, PAIRS], F32, name="y", tag="x1", bufs=1, align_bytes=64)
        for u in range(2):
            first = []
            both = []
            for t in range(2 * u, 2 * u + 2):
                take = ring.tile([P, PAIRS], F32, name="take", tag="take", bufs=2, align_bytes=64)
                nc.vector.tensor_copy(out=take[:], in_=g2[t][:].indirect(pos1_t[:]))
                first.append(take)
            for t in range(2 * u, 2 * u + 2):
                pair = ring.tile([P, PAIRS], F32, name="pair", tag="pair", bufs=2, align_bytes=64)
                nc.vector.tensor_tensor(out=pair[:], in0=g2[t][:].indirect(pos2_t[:]), in1=first[t - 2 * u][:], op=ALU.add)
                both.append(pair)
            for t in range(2 * u, 2 * u + 2):
                nc.vector.tensor_tensor(out=y[:, t, :], in0=both[t - 2 * u][:], in1=emph_t[:, t, :], op=ALU.mult)
                nc.sync.dma_start(out=out_rows[:, t, :], in_=y[:, t, :])
        rounded = []
        for mh in range(MH):
            ms = slice(mh * MW, (mh + 1) * MW)
            yb = ring.tile([P, MW, PACK], BF16, name="yb", tag="hb", bufs=2, align_bytes=64)
            dst = yb[:].rearrange("p (c i) t -> p c t i", i=4)
            src = y[:, :, ms].rearrange("p t (c i) -> p c t i", i=4)
            if mh == 0:
                nc.vector.tensor_copy(out=dst, in_=src)
            else:
                nc.scalar.copy(out=dst, in_=src)
            rounded.append(yb)
        for mh in range(MH):
            ms = slice(mh * MW, (mh + 1) * MW)
            nc.vector.quantize_mx(
                out=y_codes[:, ms].bitcast(FP8X4), scales=y_sc[:, ms], in_=rounded[mh][:].rearrange("p m t -> p (m t)")
            )
            nc.sync.dma_start(out=out_words[:, ms], in_=y_codes[:, ms].bitcast(I32))
        for q in range(4):
            queue = nc.scalar if q % 2 == 0 else nc.sync
            queue.dma_start(
                out=out_2[0, 4 * q : 4 * q + 4, :].bitcast(I32), in_=y_sc[32 * q : 32 * q + 4, :].bitcast(I32)
            )
